import numpy as np
import ml_dtypes


def mxq(x, axis, fmt="e4m3"):
    dtype, down = {"e4m3": (ml_dtypes.float8_e4m3fn, 7), "e5m2": (ml_dtypes.float8_e5m2, 14)}[fmt]
    v = np.moveaxis(np.asarray(x, np.float32).astype(ml_dtypes.bfloat16).astype(np.float64), axis, -1)
    blocks = v.reshape(v.shape[:-1] + (-1, 32))
    amax = np.abs(blocks).max(-1, keepdims=True)
    byte = np.maximum(np.where(amax > 0, np.frexp(amax)[1] - 1 + 127, 0) - down, 1)
    scale = np.exp2(byte - 127.0)
    codes = (blocks / scale).astype(np.float32).astype(dtype).astype(np.float64)
    return np.moveaxis((codes * scale).reshape(v.shape), -1, axis)


WIDE = False


def mx_kscale(k):
    if not WIDE:
        return np.ones(k)
    levels = np.array([10, -10, 5, -5, 0])
    if k % 512:
        return np.exp2(np.random.permutation(np.resize(levels, k // 32))).repeat(32)
    a = np.empty((k // 512, 16))
    for p in range(k // 512):
        a[p, :8] = np.random.permutation(np.resize(levels, 8))
        for g in range(8):
            far = levels[np.abs(levels - a[p, g]) >= 10]
            a[p, g + 8] = far[np.random.randint(len(far))]
    return np.exp2(a.ravel()).repeat(32)


def f64(x):
    return np.asarray(x).astype(np.float64)


def striped(idx):
    return np.tile(idx.reshape(-1, 16).T, (8, 1)).astype(np.uint16)


def unstriped(offs):
    return offs[:16].T.reshape(-1).astype(np.int64)


E2M1 = np.array([0.0, 0.5, 1.0, 1.5, 2.0, 3.0, 4.0, 6.0, -0.0, -0.5, -1.0, -1.5, -2.0, -3.0, -4.0, -6.0])


def pack_weight(w, fmt):
    k, n = w.shape
    w = f64(np.asarray(w, np.float32).astype(ml_dtypes.bfloat16)).reshape(k // 32, 32, n)
    amax = np.abs(w).max(1)
    if fmt == "e4m3":
        byte = np.frexp(amax)[1] - 1 + 127 - 7
    else:
        mant, ex = np.frexp(amax / 6.0)
        byte = np.where(mant > 0.5, ex, ex - 1) + 127
    byte = np.clip(np.where(amax > 0, byte, 1), 1, 254)
    scaled = (w * np.exp2(127.0 - byte)[:, None, :]).reshape(k, n).astype(np.float32)
    by_word = np.ascontiguousarray(scaled.reshape(k // 512, 128, 4, n).transpose(0, 1, 3, 2))
    if fmt == "e4m3":
        words = by_word.astype(ml_dtypes.float8_e4m3fn).view(np.uint8)
    else:
        c = by_word.astype(ml_dtypes.float4_e2m1fn).view(np.uint8) & 0xF
        words = (c[..., 0::2] | (c[..., 1::2] << 4)).reshape(k // 512, 128, 2 * n)
    return np.ascontiguousarray(words), np.ascontiguousarray(byte.astype(np.uint8).reshape(k // 512, 16, n))


def unpack_weight(words, scales, fmt):
    g, _, n = scales.shape
    words = np.ascontiguousarray(words).reshape(g, 128, n, -1)
    if fmt == "e4m3":
        vals = words.view(ml_dtypes.float8_e4m3fn).astype(np.float64)
    else:
        nib = np.empty((g, 128, n, 4), np.uint8)
        nib[..., 0::2] = words & 0xF
        nib[..., 1::2] = words >> 4
        vals = E2M1[nib]
    vals = vals * np.repeat(np.exp2(scales.astype(np.float64) - 127.0), 8, axis=1)[..., None]
    return vals.transpose(0, 1, 3, 2).reshape(g * 512, n)


K, T, E, C, N = 512, 1024, 16, 128, 256


def by_expert(wq, xq):
    return np.concatenate([wq[e].T @ xq[:, e * C:(e + 1) * C] for e in range(E)], axis=1)


def setup_inputs():
    n = np.random.standard_normal
    s = mx_kscale(K)[:, None]
    first = np.random.permutation(np.repeat(np.arange(E), T // E))
    second = (first + 1 + np.random.permutation(np.repeat(np.arange(E - 1), -(-T // (E - 1)))[:T])) % E
    while np.bincount(second, minlength=E).max() != T // E:
        load = np.bincount(second, minlength=E); hi, lo = int(load.argmax()), int(load.argmin())
        t = np.flatnonzero((second == hi) & (first != lo))[0]; second[t] = lo
    slot_token = np.empty(E * C, np.int64); pos = np.empty((2, T), np.int64); fill = np.zeros(E, np.int64)
    place = np.stack([np.random.permutation(C) for _ in range(E)])
    for r, deal in enumerate((first, second)):
        for t in np.random.permutation(T):
            e = deal[t]; j = e * C + place[e, fill[e]]; fill[e] += 1; slot_token[j] = t; pos[r, t] = j
    g = np.random.uniform(0.2, 0.8, T)
    x = pack_weight(n((K, T)) * s, "e4m3")
    return {
        "x_words": x[0],
        "x_scales": x[1],
        "w": (n((E, K, N)) / np.sqrt(K) / s[None]).astype(np.float32),
        "gate": np.stack([np.tile(g, (N, 1)), np.tile(1.0 - g, (N, 1))]).astype(np.float32),
        "offs": striped(slot_token),
        "pos1": striped(pos[0]),
        "pos2": striped(pos[1]),
    }


def reference(x_words, x_scales, w, gate, offs, pos1, pos2):
    idx = unstriped(offs)
    xq = unpack_weight(x_words, x_scales, "e4m3")[:, idx]
    y = by_expert(mxq(f64(w), 1, "e4m3"), xq)
    return f64(gate[0]) * y[:, unstriped(pos1)] + f64(gate[1]) * y[:, unstriped(pos2)]

@@ -1,0 +1,172 @@
+from contextlib import ExitStack
+
+import concourse.mybir as mybir
+from concourse.masks import make_identity
+
+K, T, E, C, N = 512, 1024, 16, 128, 256
+FLOPS = 2 * K * N * E * C
+BYTES = K * T + 16 * T + 4 * E * K * N + 2 * 4 * T + 2 * 128 * (128 + 64 + 64) + 4 * N * T
+
+F32 = mybir.dt.float32
+BF16 = mybir.dt.bfloat16
+I32 = mybir.dt.int32
+U32 = mybir.dt.uint32
+U16 = mybir.dt.uint16
+U8 = mybir.dt.uint8
+FP8X4 = mybir.dt.float8_e4m3fn_x4
+COPY = mybir.ActivationFunctionType.Copy
+MULT = mybir.AluOpType.mult
+ADD = mybir.AluOpType.add
+
+P = 128
+PACK = 4
+SLOTS = E * C
+PER_COL = 16
+GATHER = 512
+CHUNK = 256
+WHOLE = 2
+GROUPS = {
+    0: [(0, 4), (4, 8), (8, 12), (12, 16)],
+    1: [(0, 4), (4, 8), (8, 12), (12, 14), (14, 15), (15, 16)],
+}
+VECTOR_CASTS = {0: range(14, 16), 1: range(2, 16)}
+STAGED_IN_Y = 13
+GATED_OVER = [12, 13, 14, 15]
+PICKED_OVER = [None]*4
+
+
+def tile_moe_pkd_lin_none_kernel(tc, x_words, x_scales, w, gate, offs, pos1, pos2, out):
+    nc = tc.nc
+    with ExitStack() as ctx:
+        keep = ctx.enter_context(tc.tile_pool(name="keep", bufs=1))
+        gate_banks = ctx.enter_context(tc.psum_pool(name="gate_banks", bufs=1))
+        sum_banks = ctx.enter_context(tc.psum_pool(name="sum_banks", bufs=4))
+
+        offs_sb = keep.tile([P, SLOTS // PER_COL], U16, name="offs_sb")
+        pos_sb = [keep.tile([P, T // PER_COL], U16, name="pos%d_sb" % r) for r in range(2)]
+        token_words = keep.tile([P, T], I32, name="token_words")
+        token_scales = keep.tile([P, T // 4], I32, name="token_scales")
+        gate_cols = [keep.tile([P, T // CHUNK, 2], F32, name="gate_cols%d" % r) for r in range(2)]
+        ident = keep.tile([P, P], F32, name="ident")
+        y = [keep.tile([P, SLOTS], F32, name="y%d" % h) for h in range(2)]
+
+        nc.gpsimd.memset(token_scales[:], 0)
+        make_identity(nc, ident[:])
+
+        raw = {}
+
+        def load_weights(e, halves):
+            width = P * len(halves)
+            first = P * halves[0]
+            if (e, halves) == (STAGED_IN_Y, (0,)):
+                dst = y[0][:].rearrange("p (j s) -> p j s", j=PACK)[:, :, 0:P]
+            else:
+                dst = keep.tile([P, PACK, width], F32, name="raw_%d_%d" % (e, halves[0]))[:]
+            rows = w[e].rearrange("(p j) n -> p j n", j=PACK)
+            nc.sync.dma_start(out=dst, in_=rows[:, :, first : first + width])
+            for a, h in enumerate(halves):
+                raw[e, h] = dst[:, :, a * P : (a + 1) * P]
+
+        scale_rows = x_scales[0].bitcast(I32)
+        nc.sync.dma_start(offs_sb[:], offs)
+        for j in range(4):
+            queue = nc.sync if j < 2 else nc.scalar
+            queue.dma_start(out=token_scales[j:P:32, :], in_=scale_rows[j:16:4, :])
+        for e in range(E):
+            if e == 2:
+                nc.sync.dma_start(out=token_words[:], in_=x_words[0].rearrange("p t r -> p (t r)").bitcast(I32))
+            if e == 3:
+                for r in range(2):
+                    nc.sync.dma_start(out=gate_cols[r][:], in_=gate[r][0].rearrange("(c q i) -> q c i", q=P, i=2))
+            if e == 12:
+                nc.sync.dma_start(pos_sb[0][:], pos1)
+                nc.sync.dma_start(pos_sb[1][:], pos2)
+            load_weights(e, (0, 1) if e < WHOLE else (0,))
+        for e in range(WHOLE, E):
+            load_weights(e, (1,))
+
+        slot_words, slot_scales = [], []
+        for g in range(SLOTS // GATHER):
+            cols = slice(g * GATHER // PER_COL, (g + 1) * GATHER // PER_COL)
+            words = keep.tile([P, GATHER], U32, name="slot_words%d" % g, align_bytes=64)
+            scales = keep.tile([P, GATHER], U8, name="slot_scales%d" % g, align_bytes=64)
+            nc.vector.tensor_copy(scales[:], token_scales[:].bitcast(U8).indirect(offs_sb[:, cols]))
+            nc.vector.tensor_copy(words[:], token_words[:].bitcast(U32).indirect(offs_sb[:, cols]))
+            slot_words.append(words)
+            slot_scales.append(scales)
+
+        gates = []
+        for c in range(T // CHUNK):
+            bank = gate_banks.tile([P, 2, 2, P], F32, name="gates%d" % c)
+            for r in range(2):
+                for i in range(2):
+                    nc.tensor.transpose(bank[:, r, i, :], gate_cols[r][:, c, i : i + 1].to_broadcast([P, P]), ident[:])
+            gates.append(bank)
+
+        def round_weights(h, first, last):
+            rounded = keep.tile([P, (last - first) * P * PACK], BF16, name="rounded_%d_%d" % (h, first), align_bytes=64)
+            for e in range(first, last):
+                part = rounded[:, (e - first) * P * PACK : (e - first + 1) * P * PACK]
+                dst = part.rearrange("p (c i j) -> p c j i", i=4, j=PACK)
+                src = raw[e, h].rearrange("p j (c i) -> p c j i", i=4)
+                if e in VECTOR_CASTS[h]:
+                    nc.vector.tensor_copy(out=dst, in_=src)
+                else:
+                    nc.scalar.activation(dst, src, COPY)
+            return rounded
+
+        def experts(h, first, last, rounded):
+            count = last - first
+            name = "_%d_%d" % (h, first)
+            codes = keep.tile([P, count * P], U32, name="codes" + name, align_bytes=64)
+            scales = keep.tile([P, count * P], U8, name="scales" + name, align_bytes=64)
+            nc.vector.quantize_mx(out=codes[:].bitcast(FP8X4), scales=scales[:], in_=rounded[:])
+            sums = sum_banks.tile([P, count * C], F32, name="sums", tag="sums")
+            for e in range(first, last):
+                g, at = divmod(e * C, GATHER)
+                own = slice((e - first) * P, (e - first + 1) * P)
+                nc.tensor.matmul_mx(
+                    out=sums[:, own],
+                    lhsT=codes[:, own].bitcast(FP8X4),
+                    lhsT_scale=scales[:, own],
+                    rhs=slot_words[g][:, at : at + C].bitcast(FP8X4),
+                    rhs_scale=slot_scales[g][:, at : at + C],
+                    start=True,
+                    stop=True,
+                )
+            nc.scalar.activation(y[h][:, first * C : last * C], sums[:], COPY)
+
+        def pair_tile(over, name):
+            if over is None:
+                return keep.tile([P, 2, CHUNK], F32, name=name)[:]
+            return raw[over, 1].rearrange("p (r a) n -> p r (a n)", r=2)
+
+        def combine(h, c):
+            name = "_%d_%d" % (h, c)
+            cols = slice(c * CHUNK // PER_COL, (c + 1) * CHUNK // PER_COL)
+            picked = pair_tile(PICKED_OVER[c] if h == 0 else None, "picked" + name)
+            gated = pair_tile(GATED_OVER[c] if h == 0 else None, "gated" + name)
+            result = keep.tile([P, CHUNK], F32, name="result" + name)
+            for r in range(2):
+                window = y[h][:].indirect(pos_sb[r][:, cols])
+                if h == 1 and r == 1 and c in ():
+                    nc.vector.tensor_copy(picked[:, r, :], window)
+                else:
+                    nc.scalar.activation(picked[:, r, :], window, COPY)
+            nc.vector.tensor_tensor(
+                gated.rearrange("p r (q i) -> p r q i", i=2),
+                picked.rearrange("p r (q i) -> p r q i", i=2),
+                gates[c][:].rearrange("p r i q -> p r q i"),
+                MULT,
+            )
+            nc.vector.tensor_tensor(result[:], gated[:, 0, :], gated[:, 1, :], ADD)
+            nc.sync.dma_start(out=out[h * P : (h + 1) * P, c * CHUNK : (c + 1) * CHUNK], in_=result[:])
+
+        first_half = [round_weights(0, first, last) for first, last in GROUPS[0]]
+        for (first, last), rounded in zip(GROUPS[0], first_half):
+            experts(0, first, last, rounded)
+        for first, last in GROUPS[1]:
+            experts(1, first, last, round_weights(1, first, last))
+        for h in range(2):
+            for c in range(T // CHUNK):
+                combine(h, c)

@@ -24,15 +24,10 @@ SLOTS = E * C
 PER_COL = 16
 GATHER = 512
 CHUNK = 256
-WHOLE = 2
-GROUPS = {
-    0: [(0, 4), (4, 8), (8, 12), (12, 16)],
-    1: [(0, 4), (4, 8), (8, 12), (12, 14), (14, 15), (15, 16)],
-}
-VECTOR_CASTS = {0: range(14, 16), 1: range(2, 16)}
-STAGED_IN_Y = 13
-GATED_OVER = [12, 13, 14, 15]
-PICKED_OVER = [None]*4
+GROUPS = [(0, 4), (4, 8), (8, 12), (12, 14), (14, 15), (15, 16)]
+LOADS = [(e, e + 1) for e in range(16)]
+STAGED_IN_Y = {7: 0, 8: 1}
+VECTOR_GATHERS = ((0, 0), (0, 2), (0, 4))
 
 
 def tile_moe_pkd_lin_none_kernel(tc, x_words, x_scales, w, gate, offs, pos1, pos2, out):
@@ -46,44 +41,47 @@ def tile_moe_pkd_lin_none_kernel(tc, x_words, x_scales, w, gate, offs, pos1, pos
         pos_sb = [keep.tile([P, T // PER_COL], U16, name="pos%d_sb" % r) for r in range(2)]
         token_words = keep.tile([P, T], I32, name="token_words")
         token_scales = keep.tile([P, T // 4], I32, name="token_scales")
-        gate_cols = [keep.tile([P, T // CHUNK, 2], F32, name="gate_cols%d" % r) for r in range(2)]
+        gate_rows = keep.tile([P, P], F32, name="gate_rows")
+        gate_cols = keep.tile([P, 2 * T // P], F32, name="gate_cols")
         ident = keep.tile([P, P], F32, name="ident")
         y = [keep.tile([P, SLOTS], F32, name="y%d" % h) for h in range(2)]
 
         nc.gpsimd.memset(token_scales[:], 0)
+        nc.gpsimd.memset(gate_rows[:], 0.0)
         make_identity(nc, ident[:])
 
         raw = {}
 
-        def load_weights(e, halves):
-            width = P * len(halves)
-            first = P * halves[0]
-            if (e, halves) == (STAGED_IN_Y, (0,)):
-                dst = y[0][:].rearrange("p (j s) -> p j s", j=PACK)[:, :, 0:P]
+        def load_weights(first, last):
+            count = last - first
+            if first in STAGED_IN_Y:
+                flat = y[STAGED_IN_Y[first]][:, 0 : count * PACK * N]
             else:
-                dst = keep.tile([P, PACK, width], F32, name="raw_%d_%d" % (e, halves[0]))[:]
-            rows = w[e].rearrange("(p j) n -> p j n", j=PACK)
-            nc.sync.dma_start(out=dst, in_=rows[:, :, first : first + width])
-            for a, h in enumerate(halves):
-                raw[e, h] = dst[:, :, a * P : (a + 1) * P]
+                flat = keep.tile([P, count * PACK * N], F32, name="raw%d" % first)[:]
+            nc.sync.dma_start(
+                out=flat.rearrange("p (e x) -> p e x", e=count),
+                in_=w[first:last].rearrange("e (p j) n -> p e (j n)", j=PACK),
+            )
+            rows = flat.rearrange("p (e j n) -> p e j n", e=count, j=PACK)
+            for e in range(first, last):
+                for h in range(2):
+                    raw[e, h] = rows[:, e - first, :, h * P : (h + 1) * P]
 
         scale_rows = x_scales[0].bitcast(I32)
         nc.sync.dma_start(offs_sb[:], offs)
         for j in range(4):
             queue = nc.sync if j < 2 else nc.scalar
             queue.dma_start(out=token_scales[j:P:32, :], in_=scale_rows[j:16:4, :])
-        for e in range(E):
-            if e == 2:
+        for first, last in LOADS:
+            if first == 2:
                 nc.sync.dma_start(out=token_words[:], in_=x_words[0].rearrange("p t r -> p (t r)").bitcast(I32))
-            if e == 3:
-                for r in range(2):
-                    nc.sync.dma_start(out=gate_cols[r][:], in_=gate[r][0].rearrange("(c q i) -> q c i", q=P, i=2))
-            if e == 12:
+            if first == 2:
+                blocks = gate.rearrange("r n (b q) -> (r n b) q", q=P)
+                nc.sync.dma_start(out=gate_rows[0:16, :], in_=blocks[0 : 15 * 257 + 1 : 257, :])
+            if first == 10:
                 nc.sync.dma_start(pos_sb[0][:], pos1)
                 nc.sync.dma_start(pos_sb[1][:], pos2)
-            load_weights(e, (0, 1) if e < WHOLE else (0,))
-        for e in range(WHOLE, E):
-            load_weights(e, (1,))
+            load_weights(first, last)
 
         slot_words, slot_scales = [], []
         for g in range(SLOTS // GATHER):
@@ -95,32 +93,44 @@ def tile_moe_pkd_lin_none_kernel(tc, x_words, x_scales, w, gate, offs, pos1, pos
             slot_words.append(words)
             slot_scales.append(scales)
 
+        turned = sum_banks.tile([P, P], F32, name="turned", tag="sums")
+        nc.tensor.transpose(turned[:], gate_rows[:], ident[:])
+        nc.scalar.activation(gate_cols[:], turned[:, 0:16], COPY)
         gates = []
         for c in range(T // CHUNK):
-            bank = gate_banks.tile([P, 2, 2, P], F32, name="gates%d" % c)
+            bank = gate_banks.tile([P, 2, CHUNK], F32, name="gates%d" % c)
             for r in range(2):
                 for i in range(2):
-                    nc.tensor.transpose(bank[:, r, i, :], gate_cols[r][:, c, i : i + 1].to_broadcast([P, P]), ident[:])
+                    m = 8 * r + 2 * c + i
+                    nc.tensor.transpose(
+                        bank[:, r, i * P : (i + 1) * P], gate_cols[:, m : m + 1].to_broadcast([P, P]), ident[:]
+                    )
             gates.append(bank)
 
-        def round_weights(h, first, last):
-            rounded = keep.tile([P, (last - first) * P * PACK], BF16, name="rounded_%d_%d" % (h, first), align_bytes=64)
-            for e in range(first, last):
-                part = rounded[:, (e - first) * P * PACK : (e - first + 1) * P * PACK]
-                dst = part.rearrange("p (c i j) -> p c j i", i=4, j=PACK)
-                src = raw[e, h].rearrange("p j (c i) -> p c j i", i=4)
-                if e in VECTOR_CASTS[h]:
-                    nc.vector.tensor_copy(out=dst, in_=src)
-                else:
-                    nc.scalar.activation(dst, src, COPY)
-            return rounded
+        rounded = {}
+        for first, last in GROUPS:
+            for h in range(2):
+                rounded[h, first] = keep.tile(
+                    [P, (last - first) * P * PACK], BF16, name="rounded_%d_%d" % (h, first), align_bytes=64
+                )
 
-        def experts(h, first, last, rounded):
+        def round_weights(first, last):
+            for e in range(first, last):
+                for h in range(2):
+                    part = rounded[h, first][:, (e - first) * P * PACK : (e - first + 1) * P * PACK]
+                    dst = part.rearrange("p (c i j) -> p c j i", i=4, j=PACK)
+                    src = raw[e, h].rearrange("p j (c i) -> p c j i", i=4)
+                    if e >= 8 and h == (0 if e == 15 else 1):
+                        nc.vector.tensor_copy(out=dst, in_=src)
+                    else:
+                        nc.scalar.activation(dst, src, COPY)
+
+        def experts(h, first, last):
             count = last - first
             name = "_%d_%d" % (h, first)
             codes = keep.tile([P, count * P], U32, name="codes" + name, align_bytes=64)
             scales = keep.tile([P, count * P], U8, name="scales" + name, align_bytes=64)
-            nc.vector.quantize_mx(out=codes[:].bitcast(FP8X4), scales=scales[:], in_=rounded[:])
+            nc.vector.quantize_mx(out=codes[:].bitcast(FP8X4), scales=scales[:], in_=rounded[h, first][:])
             sums = sum_banks.tile([P, count * C], F32, name="sums", tag="sums")
             for e in range(first, last):
                 g, at = divmod(e * C, GATHER)
@@ -136,37 +146,33 @@ def tile_moe_pkd_lin_none_kernel(tc, x_words, x_scales, w, gate, offs, pos1, pos
                 )
             nc.scalar.activation(y[h][:, first * C : last * C], sums[:], COPY)
 
-        def pair_tile(over, name):
-            if over is None:
-                return keep.tile([P, 2, CHUNK], F32, name=name)[:]
-            return raw[over, 1].rearrange("p (r a) n -> p r (a n)", r=2)
-
-        def combine(h, c):
-            name = "_%d_%d" % (h, c)
-            cols = slice(c * CHUNK // PER_COL, (c + 1) * CHUNK // PER_COL)
-            picked = pair_tile(PICKED_OVER[c] if h == 0 else None, "picked" + name)
-            gated = pair_tile(GATED_OVER[c] if h == 0 else None, "gated" + name)
-            result = keep.tile([P, CHUNK], F32, name="result" + name)
+        def combine(h, start, size):
+            name = "_%d_%d" % (h, start)
+            cols = slice(start // PER_COL, (start + size) // PER_COL)
+            c, at = divmod(start, CHUNK)
+            picked = keep.tile([P, 2, size], F32, name="picked" + name)
+            gated = keep.tile([P, 2, size], F32, name="gated" + name)
+            result = keep.tile([P, size], F32, name="result" + name)
             for r in range(2):
                 window = y[h][:].indirect(pos_sb[r][:, cols])
-                if h == 1 and r == 1 and c in ():
+                if r == 1 and (h, start // P) in VECTOR_GATHERS:
                     nc.vector.tensor_copy(picked[:, r, :], window)
                 else:
                     nc.scalar.activation(picked[:, r, :], window, COPY)
-            nc.vector.tensor_tensor(
-                gated.rearrange("p r (q i) -> p r q i", i=2),
-                picked.rearrange("p r (q i) -> p r q i", i=2),
-                gates[c][:].rearrange("p r i q -> p r q i"),
-                MULT,
-            )
-            nc.vector.tensor_tensor(result[:], gated[:, 0, :], gated[:, 1, :], ADD)
-            nc.sync.dma_start(out=out[h * P : (h + 1) * P, c * CHUNK : (c + 1) * CHUNK], in_=result[:])
+            nc.vector.tensor_tensor(gated[:], picked[:], gates[c][:, :, at : at + size], MULT)
+            adder = nc.gpsimd if False else nc.vector
+            adder.tensor_tensor(result[:], gated[:, 0, :], gated[:, 1, :], ADD)
+            nc.sync.dma_start(out=out[h * P : (h + 1) * P, start : start + size], in_=result[:])
 
-        first_half = [round_weights(0, first, last) for first, last in GROUPS[0]]
-        for (first, last), rounded in zip(GROUPS[0], first_half):
-            experts(0, first, last, rounded)
-        for first, last in GROUPS[1]:
-            experts(1, first, last, round_weights(1, first, last))
-        for h in range(2):
-            for c in range(T // CHUNK):
-                combine(h, c)
+        for first, last in GROUPS[:3]:
+            round_weights(first, last)
+        for first, last in GROUPS[:3]:
+            for h in range(2):
+                experts(h, first, last)
+        for first, last in GROUPS[3:]:
+            round_weights(first, last)
+            for h in range(2):
+                experts(h, first, last)
+        for h, chunks in enumerate(([(c * CHUNK, CHUNK) for c in range(4)], [(0, 256), (256, 256), (512, 256), (768, 128), (896, 128)])):
+            for start, size in chunks:
+                combine(h, start, size)

@@ -5,7 +5,7 @@ from concourse.masks import make_identity
 
 K, T, E, C, N = 512, 1024, 16, 128, 256
 FLOPS = 2 * K * N * E * C
-BYTES = K * T + 16 * T + 4 * E * K * N + 2 * 4 * T + 2 * 128 * (128 + 64 + 64) + 4 * N * T
+BYTES = K * T + (K // 32) * T + 4 * E * K * N + 2 * 4 * T + 2 * 128 * (128 + 64 + 64) + 4 * N * T
 
 F32 = mybir.dt.float32
 BF16 = mybir.dt.bfloat16
@@ -20,14 +20,20 @@ ADD = mybir.AluOpType.add
 
 P = 128
 PACK = 4
+LINE = 4
 SLOTS = E * C
-PER_COL = 16
-GATHER = 512
-CHUNK = 256
-GROUPS = [(0, 4), (4, 8), (8, 12), (12, 14), (14, 15), (15, 16)]
-LOADS = [(e, e + 1) for e in range(16)]
-STAGED_IN_Y = {7: 0, 8: 1}
-VECTOR_GATHERS = ((0, 0), (0, 2), (0, 4))
+ENTRIES = 16
+BANK = 512
+PER_BANK = BANK // C
+CHUNK = BANK // 2
+GATE_BLOCKS = 2 * T // P
+
+FULL_GROUPS = [(e, e + PER_BANK) for e in range(0, E, PER_BANK)]
+GROUPS = (FULL_GROUPS[:-1] + [(E - PER_BANK, E - 2), (E - 2, E - 1), (E - 1, E)], FULL_GROUPS)
+
+SHARED_FROM = 8
+HELPED_CHUNKS = 5
+WORDS_BEFORE, POSITIONS_BEFORE = 2, 10
 
 
 def tile_moe_pkd_lin_none_kernel(tc, x_words, x_scales, w, gate, offs, pos1, pos2, out):
@@ -37,12 +43,12 @@ def tile_moe_pkd_lin_none_kernel(tc, x_words, x_scales, w, gate, offs, pos1, pos
         gate_banks = ctx.enter_context(tc.psum_pool(name="gate_banks", bufs=1))
         sum_banks = ctx.enter_context(tc.psum_pool(name="sum_banks", bufs=4))
 
-        offs_sb = keep.tile([P, SLOTS // PER_COL], U16, name="offs_sb")
-        pos_sb = [keep.tile([P, T // PER_COL], U16, name="pos%d_sb" % r) for r in range(2)]
+        offs_sb = keep.tile([P, SLOTS // ENTRIES], U16, name="offs_sb")
+        pos_sb = [keep.tile([P, T // ENTRIES], U16, name="pos%d_sb" % r) for r in range(2)]
         token_words = keep.tile([P, T], I32, name="token_words")
         token_scales = keep.tile([P, T // 4], I32, name="token_scales")
         gate_rows = keep.tile([P, P], F32, name="gate_rows")
-        gate_cols = keep.tile([P, 2 * T // P], F32, name="gate_cols")
+        gate_cols = keep.tile([P, GATE_BLOCKS], F32, name="gate_cols")
         ident = keep.tile([P, P], F32, name="ident")
         y = [keep.tile([P, SLOTS], F32, name="y%d" % h) for h in range(2)]
 
@@ -50,82 +56,80 @@ def tile_moe_pkd_lin_none_kernel(tc, x_words, x_scales, w, gate, offs, pos1, pos
         nc.gpsimd.memset(gate_rows[:], 0.0)
         make_identity(nc, ident[:])
 
+        staged_in_y = {SHARED_FROM - 1: y[0], SHARED_FROM: y[1]}
         raw = {}
 
-        def load_weights(first, last):
-            count = last - first
-            if first in STAGED_IN_Y:
-                flat = y[STAGED_IN_Y[first]][:, 0 : count * PACK * N]
+        def load_weights(e):
+            if e in staged_in_y:
+                flat = staged_in_y[e][:, 0 : PACK * N]
             else:
-                flat = keep.tile([P, count * PACK * N], F32, name="raw%d" % first)[:]
-            nc.sync.dma_start(
-                out=flat.rearrange("p (e x) -> p e x", e=count),
-                in_=w[first:last].rearrange("e (p j) n -> p e (j n)", j=PACK),
-            )
-            rows = flat.rearrange("p (e j n) -> p e j n", e=count, j=PACK)
-            for e in range(first, last):
-                for h in range(2):
-                    raw[e, h] = rows[:, e - first, :, h * P : (h + 1) * P]
+                flat = keep.tile([P, PACK * N], F32, name="raw%d" % e)[:]
+            nc.sync.dma_start(out=flat, in_=w[e].rearrange("(p j) n -> p (j n)", j=PACK))
+            rows = flat.rearrange("p (j n) -> p j n", j=PACK)
+            for h in range(2):
+                raw[e, h] = rows[:, :, h * P : (h + 1) * P]
 
         scale_rows = x_scales[0].bitcast(I32)
         nc.sync.dma_start(offs_sb[:], offs)
         for j in range(4):
             queue = nc.sync if j < 2 else nc.scalar
-            queue.dma_start(out=token_scales[j:P:32, :], in_=scale_rows[j:16:4, :])
-        for first, last in LOADS:
-            if first == 2:
+            queue.dma_start(out=token_scales[j:P:32, :], in_=scale_rows[j : K // 32 : 4, :])
+        for e in range(E):
+            if e == WORDS_BEFORE:
                 nc.sync.dma_start(out=token_words[:], in_=x_words[0].rearrange("p t r -> p (t r)").bitcast(I32))
-            if first == 2:
                 blocks = gate.rearrange("r n (b q) -> (r n b) q", q=P)
-                nc.sync.dma_start(out=gate_rows[0:16, :], in_=blocks[0 : 15 * 257 + 1 : 257, :])
-            if first == 10:
+                step = 32 * (T // P) + 1
+                nc.sync.dma_start(
+                    out=gate_rows[0:GATE_BLOCKS, :], in_=blocks[0 : (GATE_BLOCKS - 1) * step + 1 : step, :]
+                )
+            if e == POSITIONS_BEFORE:
                 nc.sync.dma_start(pos_sb[0][:], pos1)
                 nc.sync.dma_start(pos_sb[1][:], pos2)
-            load_weights(first, last)
+            load_weights(e)
 
         slot_words, slot_scales = [], []
-        for g in range(SLOTS // GATHER):
-            cols = slice(g * GATHER // PER_COL, (g + 1) * GATHER // PER_COL)
-            words = keep.tile([P, GATHER], U32, name="slot_words%d" % g, align_bytes=64)
-            scales = keep.tile([P, GATHER], U8, name="slot_scales%d" % g, align_bytes=64)
-            nc.vector.tensor_copy(scales[:], token_scales[:].bitcast(U8).indirect(offs_sb[:, cols]))
-            nc.vector.tensor_copy(words[:], token_words[:].bitcast(U32).indirect(offs_sb[:, cols]))
+        for g in range(SLOTS // BANK):
+            entries = offs_sb[:, g * BANK // ENTRIES : (g + 1) * BANK // ENTRIES]
+            words = keep.tile([P, BANK], U32, name="slot_words%d" % g, align_bytes=64)
+            scale_bytes = keep.tile([P, BANK], U8, name="slot_scales%d" % g, align_bytes=64)
+            nc.vector.tensor_copy(scale_bytes[:], token_scales[:].bitcast(U8).indirect(entries))
+            nc.vector.tensor_copy(words[:], token_words[:].bitcast(U32).indirect(entries))
             slot_words.append(words)
-            slot_scales.append(scales)
+            slot_scales.append(scale_bytes)
 
         turned = sum_banks.tile([P, P], F32, name="turned", tag="sums")
         nc.tensor.transpose(turned[:], gate_rows[:], ident[:])
-        nc.scalar.activation(gate_cols[:], turned[:, 0:16], COPY)
+        nc.scalar.activation(gate_cols[:], turned[:, 0:GATE_BLOCKS], COPY)
         gates = []
         for c in range(T // CHUNK):
             bank = gate_banks.tile([P, 2, CHUNK], F32, name="gates%d" % c)
             for r in range(2):
-                for i in range(2):
-                    m = 8 * r + 2 * c + i
+                for i in range(CHUNK // P):
+                    block = r * (T // P) + c * (CHUNK // P) + i
                     nc.tensor.transpose(
-                        bank[:, r, i * P : (i + 1) * P], gate_cols[:, m : m + 1].to_broadcast([P, P]), ident[:]
+                        bank[:, r, i * P : (i + 1) * P], gate_cols[:, block : block + 1].to_broadcast([P, P]), ident[:]
                     )
             gates.append(bank)
 
         rounded = {}
-        for first, last in GROUPS:
-            for h in range(2):
+        for h in range(2):
+            for first, last in GROUPS[h]:
                 rounded[h, first] = keep.tile(
                     [P, (last - first) * P * PACK], BF16, name="rounded_%d_%d" % (h, first), align_bytes=64
                 )
 
-        def round_weights(first, last):
-            for e in range(first, last):
-                for h in range(2):
-                    part = rounded[h, first][:, (e - first) * P * PACK : (e - first + 1) * P * PACK]
-                    dst = part.rearrange("p (c i j) -> p c j i", i=4, j=PACK)
-                    src = raw[e, h].rearrange("p j (c i) -> p c j i", i=4)
-                    if e >= 8 and h == (0 if e == 15 else 1):
-                        nc.vector.tensor_copy(out=dst, in_=src)
-                    else:
-                        nc.scalar.activation(dst, src, COPY)
+        def round_weights(e):
+            for h in range(2):
+                first = max(f for f, last in GROUPS[h] if f <= e)
+                part = rounded[h, first][:, (e - first) * P * PACK : (e - first + 1) * P * PACK]
+                dst = part.rearrange("p (a i j) -> p a j i", i=LINE, j=PACK)
+                src = raw[e, h].rearrange("p j (a i) -> p a j i", i=LINE)
+                if e >= SHARED_FROM and (h == 0 or (e % 2 == 1 and e < E - 1)):
+                    nc.vector.tensor_copy(out=dst, in_=src)
+                else:
+                    nc.scalar.activation(dst, src, COPY)
 
-        def experts(h, first, last):
+        def multiply(h, first, last):
             count = last - first
             name = "_%d_%d" % (h, first)
             codes = keep.tile([P, count * P], U32, name="codes" + name, align_bytes=64)
@@ -133,7 +137,7 @@ def tile_moe_pkd_lin_none_kernel(tc, x_words, x_scales, w, gate, offs, pos1, pos
             nc.vector.quantize_mx(out=codes[:].bitcast(FP8X4), scales=scales[:], in_=rounded[h, first][:])
             sums = sum_banks.tile([P, count * C], F32, name="sums", tag="sums")
             for e in range(first, last):
-                g, at = divmod(e * C, GATHER)
+                g, at = divmod(e * C, BANK)
                 own = slice((e - first) * P, (e - first + 1) * P)
                 nc.tensor.matmul_mx(
                     out=sums[:, own],
@@ -146,33 +150,36 @@ def tile_moe_pkd_lin_none_kernel(tc, x_words, x_scales, w, gate, offs, pos1, pos
                 )
             nc.scalar.activation(y[h][:, first * C : last * C], sums[:], COPY)
 
-        def combine(h, start, size):
+        def combine(h, start, size, helped):
             name = "_%d_%d" % (h, start)
-            cols = slice(start // PER_COL, (start + size) // PER_COL)
+            columns = slice(start // ENTRIES, (start + size) // ENTRIES)
             c, at = divmod(start, CHUNK)
             picked = keep.tile([P, 2, size], F32, name="picked" + name)
             gated = keep.tile([P, 2, size], F32, name="gated" + name)
             result = keep.tile([P, size], F32, name="result" + name)
             for r in range(2):
-                window = y[h][:].indirect(pos_sb[r][:, cols])
-                if r == 1 and (h, start // P) in VECTOR_GATHERS:
+                window = y[h][:].indirect(pos_sb[r][:, columns])
+                if helped and r == 1:
                     nc.vector.tensor_copy(picked[:, r, :], window)
                 else:
                     nc.scalar.activation(picked[:, r, :], window, COPY)
             nc.vector.tensor_tensor(gated[:], picked[:], gates[c][:, :, at : at + size], MULT)
-            adder = nc.gpsimd if False else nc.vector
+            adder = nc.gpsimd if helped else nc.vector
             adder.tensor_tensor(result[:], gated[:, 0, :], gated[:, 1, :], ADD)
             nc.sync.dma_start(out=out[h * P : (h + 1) * P, start : start + size], in_=result[:])
 
-        for first, last in GROUPS[:3]:
-            round_weights(first, last)
-        for first, last in GROUPS[:3]:
+        early = max(staged_in_y) + 1
+        for e in range(early):
+            round_weights(e)
+        for e in range(E):
+            if e >= early:
+                round_weights(e)
             for h in range(2):
-                experts(h, first, last)
-        for first, last in GROUPS[3:]:
-            round_weights(first, last)
-            for h in range(2):
-                experts(h, first, last)
-        for h, chunks in enumerate(([(c * CHUNK, CHUNK) for c in range(4)], [(0, 256), (256, 256), (512, 256), (768, 128), (896, 128)])):
-            for start, size in chunks:
-                combine(h, start, size)
+                for first, last in GROUPS[h]:
+                    if last == e + 1:
+                        multiply(h, first, last)
+
+        pieces = [(h, start, CHUNK) for h in range(2) for start in range(0, T, CHUNK)]
+        pieces = pieces[:-1] + [(1, T - CHUNK, CHUNK // 2), (1, T - CHUNK // 2, CHUNK // 2)]
+        for number, (h, start, size) in enumerate(pieces):
+            combine(h, start, size, number < HELPED_CHUNKS)

from contextlib import ExitStack

import concourse.mybir as mybir
from concourse.masks import make_identity

K, T, E, C, N = 512, 1024, 16, 128, 256
FLOPS = 2 * K * N * E * C
BYTES = K * T + (K // 32) * T + 4 * E * K * N + 2 * 4 * T + 2 * 128 * (128 + 64 + 64) + 4 * N * T

F32 = mybir.dt.float32
BF16 = mybir.dt.bfloat16
I32 = mybir.dt.int32
U32 = mybir.dt.uint32
U16 = mybir.dt.uint16
U8 = mybir.dt.uint8
FP8X4 = mybir.dt.float8_e4m3fn_x4
COPY = mybir.ActivationFunctionType.Copy
MULT = mybir.AluOpType.mult
ADD = mybir.AluOpType.add

P = 128
PACK = 4
LINE = 4
SLOTS = E * C
ENTRIES = 16
BANK = 512
PER_BANK = BANK // C
CHUNK = BANK // 2
GATE_BLOCKS = 2 * T // P

FULL_GROUPS = [(e, e + PER_BANK) for e in range(0, E, PER_BANK)]
GROUPS = (FULL_GROUPS[:-1] + [(E - PER_BANK, E - 2), (E - 2, E - 1), (E - 1, E)], FULL_GROUPS)

SHARED_FROM = 8
HELPED_CHUNKS = 5
WORDS_BEFORE, POSITIONS_BEFORE = 2, 10


def tile_moe_pkd_lin_none_kernel(tc, x_words, x_scales, w, gate, offs, pos1, pos2, out):
    nc = tc.nc
    with ExitStack() as ctx:
        keep = ctx.enter_context(tc.tile_pool(name="keep", bufs=1))
        gate_banks = ctx.enter_context(tc.psum_pool(name="gate_banks", bufs=1))
        sum_banks = ctx.enter_context(tc.psum_pool(name="sum_banks", bufs=4))

        offs_sb = keep.tile([P, SLOTS // ENTRIES], U16, name="offs_sb")
        pos_sb = [keep.tile([P, T // ENTRIES], U16, name="pos%d_sb" % r) for r in range(2)]
        token_words = keep.tile([P, T], I32, name="token_words")
        token_scales = keep.tile([P, T // 4], I32, name="token_scales")
        gate_rows = keep.tile([P, P], F32, name="gate_rows")
        gate_cols = keep.tile([P, GATE_BLOCKS], F32, name="gate_cols")
        ident = keep.tile([P, P], F32, name="ident")
        y = [keep.tile([P, SLOTS], F32, name="y%d" % h) for h in range(2)]

        nc.gpsimd.memset(token_scales[:], 0)
        nc.gpsimd.memset(gate_rows[:], 0.0)
        make_identity(nc, ident[:])

        staged_in_y = {SHARED_FROM - 1: y[0], SHARED_FROM: y[1]}
        raw = {}

        def load_weights(e):
            if e in staged_in_y:
                flat = staged_in_y[e][:, 0 : PACK * N]
            else:
                flat = keep.tile([P, PACK * N], F32, name="raw%d" % e)[:]
            nc.sync.dma_start(out=flat, in_=w[e].rearrange("(p j) n -> p (j n)", j=PACK))
            rows = flat.rearrange("p (j n) -> p j n", j=PACK)
            for h in range(2):
                raw[e, h] = rows[:, :, h * P : (h + 1) * P]

        scale_rows = x_scales[0].bitcast(I32)
        nc.sync.dma_start(offs_sb[:], offs)
        for j in range(4):
            queue = nc.sync if j < 2 else nc.scalar
            queue.dma_start(out=token_scales[j:P:32, :], in_=scale_rows[j : K // 32 : 4, :])
        for e in range(E):
            if e == WORDS_BEFORE:
                nc.sync.dma_start(out=token_words[:], in_=x_words[0].rearrange("p t r -> p (t r)").bitcast(I32))
                blocks = gate.rearrange("r n (b q) -> (r n b) q", q=P)
                step = 32 * (T // P) + 1
                nc.sync.dma_start(
                    out=gate_rows[0:GATE_BLOCKS, :], in_=blocks[0 : (GATE_BLOCKS - 1) * step + 1 : step, :]
                )
            if e == POSITIONS_BEFORE:
                nc.sync.dma_start(pos_sb[0][:], pos1)
                nc.sync.dma_start(pos_sb[1][:], pos2)
            load_weights(e)

        slot_words, slot_scales = [], []
        for g in range(SLOTS // BANK):
            entries = offs_sb[:, g * BANK // ENTRIES : (g + 1) * BANK // ENTRIES]
            words = keep.tile([P, BANK], U32, name="slot_words%d" % g, align_bytes=64)
            scale_bytes = keep.tile([P, BANK], U8, name="slot_scales%d" % g, align_bytes=64)
            nc.vector.tensor_copy(scale_bytes[:], token_scales[:].bitcast(U8).indirect(entries))
            nc.vector.tensor_copy(words[:], token_words[:].bitcast(U32).indirect(entries))
            slot_words.append(words)
            slot_scales.append(scale_bytes)

        turned = sum_banks.tile([P, P], F32, name="turned", tag="sums")
        nc.tensor.transpose(turned[:], gate_rows[:], ident[:])
        nc.scalar.activation(gate_cols[:], turned[:, 0:GATE_BLOCKS], COPY)
        gates = []
        for c in range(T // CHUNK):
            bank = gate_banks.tile([P, 2, CHUNK], F32, name="gates%d" % c)
            for r in range(2):
                for i in range(CHUNK // P):
                    block = r * (T // P) + c * (CHUNK // P) + i
                    nc.tensor.transpose(
                        bank[:, r, i * P : (i + 1) * P], gate_cols[:, block : block + 1].to_broadcast([P, P]), ident[:]
                    )
            gates.append(bank)

        rounded = {}
        for h in range(2):
            for first, last in GROUPS[h]:
                rounded[h, first] = keep.tile(
                    [P, (last - first) * P * PACK], BF16, name="rounded_%d_%d" % (h, first), align_bytes=64
                )

        def round_weights(e):
            for h in range(2):
                first = max(f for f, last in GROUPS[h] if f <= e)
                part = rounded[h, first][:, (e - first) * P * PACK : (e - first + 1) * P * PACK]
                dst = part.rearrange("p (a i j) -> p a j i", i=LINE, j=PACK)
                src = raw[e, h].rearrange("p j (a i) -> p a j i", i=LINE)
                if e >= SHARED_FROM and (h == 0 or (e % 2 == 1 and e < E - 1)):
                    nc.vector.tensor_copy(out=dst, in_=src)
                else:
                    nc.scalar.activation(dst, src, COPY)

        def multiply(h, first, last):
            count = last - first
            name = "_%d_%d" % (h, first)
            codes = keep.tile([P, count * P], U32, name="codes" + name, align_bytes=64)
            scales = keep.tile([P, count * P], U8, name="scales" + name, align_bytes=64)
            nc.vector.quantize_mx(out=codes[:].bitcast(FP8X4), scales=scales[:], in_=rounded[h, first][:])
            sums = sum_banks.tile([P, count * C], F32, name="sums", tag="sums")
            for e in range(first, last):
                g, at = divmod(e * C, BANK)
                own = slice((e - first) * P, (e - first + 1) * P)
                nc.tensor.matmul_mx(
                    out=sums[:, own],
                    lhsT=codes[:, own].bitcast(FP8X4),
                    lhsT_scale=scales[:, own],
                    rhs=slot_words[g][:, at : at + C].bitcast(FP8X4),
                    rhs_scale=slot_scales[g][:, at : at + C],
                    start=True,
                    stop=True,
                )
            nc.scalar.activation(y[h][:, first * C : last * C], sums[:], COPY)

        def combine(h, start, size, helped):
            name = "_%d_%d" % (h, start)
            columns = slice(start // ENTRIES, (start + size) // ENTRIES)
            c, at = divmod(start, CHUNK)
            picked = keep.tile([P, 2, size], F32, name="picked" + name)
            gated = keep.tile([P, 2, size], F32, name="gated" + name)
            result = keep.tile([P, size], F32, name="result" + name)
            for r in range(2):
                window = y[h][:].indirect(pos_sb[r][:, columns])
                if helped and r == 1:
                    nc.vector.tensor_copy(picked[:, r, :], window)
                else:
                    nc.scalar.activation(picked[:, r, :], window, COPY)
            nc.vector.tensor_tensor(gated[:], picked[:], gates[c][:, :, at : at + size], MULT)
            adder = nc.gpsimd if helped else nc.vector
            adder.tensor_tensor(result[:], gated[:, 0, :], gated[:, 1, :], ADD)
            nc.sync.dma_start(out=out[h * P : (h + 1) * P, start : start + size], in_=result[:])

        early = max(staged_in_y) + 1
        for e in range(early):
            round_weights(e)
        for e in range(E):
            if e >= early:
                round_weights(e)
            for h in range(2):
                for first, last in GROUPS[h]:
                    if last == e + 1:
                        multiply(h, first, last)

        pieces = [(h, start, CHUNK) for h in range(2) for start in range(0, T, CHUNK)]
        pieces = pieces[:-1] + [(1, T - CHUNK, CHUNK // 2), (1, T - CHUNK // 2, CHUNK // 2)]
        for number, (h, start, size) in enumerate(pieces):
            combine(h, start, size, number < HELPED_CHUNKS)
